import numpy as np
import ml_dtypes

BF16 = ml_dtypes.bfloat16


def bf(x):
    return np.asarray(x, np.float32).astype(BF16)


def f32(x):
    return np.asarray(x, np.float32)


def f64(x):
    return np.asarray(x).astype(np.float64)


def striped(idx):
    return np.concatenate([l.reshape(-1, 16).T for l in idx])


def rows(idx, k):
    return np.tile(np.repeat(idx, 16, axis=0), (k // (16 * 8), 1))


def look(tab, idx):
    return np.take_along_axis(f64(tab), rows(idx, len(tab)), axis=1)


K, S, V, N = 128, 2048, 2048, 2048


def setup_inputs():
    return {"tab": f32(np.random.standard_normal((2, K, S))), "y": f32(np.random.standard_normal((K, V))), "offs": striped(np.stack([np.random.permutation(S)[:N] for _ in range(8)]))}


def reference(tab, y, offs):
    idx = np.stack([g.T.reshape(-1) for g in np.split(offs, 8)])
    x = (np.minimum(look(tab[0], idx), f64(y))) * (np.tanh(look(tab[1], idx)))
    return x

@@ -1,0 +1,32 @@
+import concourse.mybir as mybir
+
+F32 = mybir.dt.float32
+U16 = mybir.dt.uint16
+LANES = 16
+PIECE = 512
+
+
+def tile_lookup_vg_mintanh_out_kernel(tc, tab, y, offs, out):
+    nc = tc.nc
+    rows, n = y.shape
+    places = tab.shape[2]
+    with tc.tile_pool(name="held", bufs=1) as held:
+        offsets = held.tile([rows, n // LANES], U16, name="offsets")
+        values = held.tile([rows, places], F32, name="values")
+        gates = held.tile([rows, places], F32, name="gates")
+        stream = held.tile([rows, n], F32, name="stream")
+        nc.sync.dma_start(offsets[:], offs)
+        nc.sync.dma_start(values[:], tab[0])
+        nc.sync.dma_start(gates[:], tab[1])
+        nc.sync.dma_start(stream[:], y)
+
+        for piece in range(n // PIECE):
+            cols = slice(piece * PIECE, (piece + 1) * PIECE)
+            entries = offsets[:, piece * PIECE // LANES : (piece + 1) * PIECE // LANES]
+            smaller = held.tile([rows, PIECE], F32, name="smaller%d" % piece)
+            gate = held.tile([rows, PIECE], F32, name="gate%d" % piece)
+            product = held.tile([rows, PIECE], F32, name="product%d" % piece)
+            nc.vector.tensor_tensor(smaller[:], values[:].indirect(entries), stream[:, cols], mybir.AluOpType.min)
+            nc.scalar.activation(gate[:], gates[:].indirect(entries), mybir.ActivationFunctionType.Tanh)
+            nc.vector.tensor_tensor(product[:], smaller[:], gate[:], mybir.AluOpType.mult)
+            nc.sync.dma_start(out[:, cols], product[:])

@@ -2,6 +2,7 @@ import concourse.mybir as mybir
 
 F32 = mybir.dt.float32
 U16 = mybir.dt.uint16
+TANH = mybir.ActivationFunctionType.Tanh
 LANES = 16
 PIECE = 512
 
@@ -10,23 +11,49 @@ def tile_lookup_vg_mintanh_out_kernel(tc, tab, y, offs, out):
     nc = tc.nc
     rows, n = y.shape
     places = tab.shape[2]
+    pieces = n // PIECE
+    half = n // 2
     with tc.tile_pool(name="held", bufs=1) as held:
         offsets = held.tile([rows, n // LANES], U16, name="offsets")
         values = held.tile([rows, places], F32, name="values")
         gates = held.tile([rows, places], F32, name="gates")
         stream = held.tile([rows, n], F32, name="stream")
-        nc.sync.dma_start(offsets[:], offs)
-        nc.sync.dma_start(values[:], tab[0])
-        nc.sync.dma_start(gates[:], tab[1])
-        nc.sync.dma_start(stream[:], y)
+        smaller = held.tile([rows, n], F32, name="smaller")
+        gate = held.tile([rows, n], F32, name="gate")
+        product = held.tile([rows, n], F32, name="product")
 
-        for piece in range(n // PIECE):
-            cols = slice(piece * PIECE, (piece + 1) * PIECE)
-            entries = offsets[:, piece * PIECE // LANES : (piece + 1) * PIECE // LANES]
-            smaller = held.tile([rows, PIECE], F32, name="smaller%d" % piece)
-            gate = held.tile([rows, PIECE], F32, name="gate%d" % piece)
-            product = held.tile([rows, PIECE], F32, name="product%d" % piece)
-            nc.vector.tensor_tensor(smaller[:], values[:].indirect(entries), stream[:, cols], mybir.AluOpType.min)
-            nc.scalar.activation(gate[:], gates[:].indirect(entries), mybir.ActivationFunctionType.Tanh)
-            nc.vector.tensor_tensor(product[:], smaller[:], gate[:], mybir.AluOpType.mult)
-            nc.sync.dma_start(out[:, cols], product[:])
+        def cols(piece):
+            return slice(piece * PIECE, (piece + 1) * PIECE)
+
+        def entries(piece):
+            return offsets[:, piece * PIECE // LANES : (piece + 1) * PIECE // LANES]
+
+        nc.sync.dma_start(values[:], tab[0])
+        nc.sync.dma_start(offsets[:], offs)
+        nc.sync.dma_start(stream[:, :half], y[:, :half])
+        nc.sync.dma_start(gates[:], tab[1])
+        for piece in range(pieces // 2, pieces):
+            nc.sync.dma_start(stream[:, cols(piece)], y[:, cols(piece)])
+
+        zero = held.tile([rows, 1], F32, name="zero")
+        warm = held.tile([rows, 1], F32, name="warm")
+        nc.vector.memset(zero[:], 0.0)
+        nc.scalar.activation(warm[:], zero[:], TANH)
+
+        def minimum(piece):
+            nc.vector.tensor_tensor(smaller[:, cols(piece)], values[:].indirect(entries(piece)),
+                                    stream[:, cols(piece)], mybir.AluOpType.min)
+
+        def multiply_and_store(piece):
+            nc.vector.tensor_tensor(product[:, cols(piece)], smaller[:, cols(piece)], gate[:, cols(piece)],
+                                    mybir.AluOpType.mult)
+            nc.sync.dma_start(out[:, cols(piece)], product[:, cols(piece)])
+
+        for piece in range(pieces):
+            nc.scalar.activation(gate[:, cols(piece)], gates[:].indirect(entries(piece)), TANH)
+        for piece in range(pieces - 1):
+            minimum(piece)
+        multiply_and_store(0)
+        minimum(pieces - 1)
+        for piece in range(1, pieces):
+            multiply_and_store(piece)

@@ -44,16 +44,17 @@ def tile_lookup_vg_mintanh_out_kernel(tc, tab, y, offs, out):
             nc.vector.tensor_tensor(smaller[:, cols(piece)], values[:].indirect(entries(piece)),
                                     stream[:, cols(piece)], mybir.AluOpType.min)
 
-        def multiply_and_store(piece):
-            nc.vector.tensor_tensor(product[:, cols(piece)], smaller[:, cols(piece)], gate[:, cols(piece)],
-                                    mybir.AluOpType.mult)
-            nc.sync.dma_start(out[:, cols(piece)], product[:, cols(piece)])
+        def multiply_and_store(span):
+            nc.vector.tensor_tensor(product[:, span], smaller[:, span], gate[:, span], mybir.AluOpType.mult)
+            nc.sync.dma_start(out[:, span], product[:, span])
 
         for piece in range(pieces):
             nc.scalar.activation(gate[:, cols(piece)], gates[:].indirect(entries(piece)), TANH)
         for piece in range(pieces - 1):
             minimum(piece)
-        multiply_and_store(0)
+        multiply_and_store(cols(0))
         minimum(pieces - 1)
-        for piece in range(1, pieces):
-            multiply_and_store(piece)
+        for piece in range(1, pieces - 1):
+            multiply_and_store(cols(piece))
+        multiply_and_store(slice(n - PIECE, n - PIECE // 2))
+        multiply_and_store(slice(n - PIECE // 2, n))

@@ -5,14 +5,15 @@ U16 = mybir.dt.uint16
 TANH = mybir.ActivationFunctionType.Tanh
 LANES = 16
 PIECE = 512
+EARLY = 768
 
 
 def tile_lookup_vg_mintanh_out_kernel(tc, tab, y, offs, out):
     nc = tc.nc
     rows, n = y.shape
     places = tab.shape[2]
-    pieces = n // PIECE
-    half = n // 2
+    pieces = [slice(start, start + PIECE) for start in range(0, n, PIECE)]
+    early, middle, late = slice(0, EARLY), slice(EARLY, EARLY + PIECE), slice(EARLY + PIECE, n)
     with tc.tile_pool(name="held", bufs=1) as held:
         offsets = held.tile([rows, n // LANES], U16, name="offsets")
         values = held.tile([rows, places], F32, name="values")
@@ -22,39 +23,36 @@ def tile_lookup_vg_mintanh_out_kernel(tc, tab, y, offs, out):
         gate = held.tile([rows, n], F32, name="gate")
         product = held.tile([rows, n], F32, name="product")
 
-        def cols(piece):
-            return slice(piece * PIECE, (piece + 1) * PIECE)
-
-        def entries(piece):
-            return offsets[:, piece * PIECE // LANES : (piece + 1) * PIECE // LANES]
+        def entries(span):
+            return offsets[:, span.start // LANES : span.stop // LANES]
 
         nc.sync.dma_start(values[:], tab[0])
         nc.sync.dma_start(offsets[:], offs)
-        nc.sync.dma_start(stream[:, :half], y[:, :half])
+        nc.sync.dma_start(stream[:, early], y[:, early])
         nc.sync.dma_start(gates[:], tab[1])
-        for piece in range(pieces // 2, pieces):
-            nc.sync.dma_start(stream[:, cols(piece)], y[:, cols(piece)])
+        nc.sync.dma_start(stream[:, middle], y[:, middle])
+        nc.sync.dma_start(stream[:, late], y[:, late])
 
         zero = held.tile([rows, 1], F32, name="zero")
         warm = held.tile([rows, 1], F32, name="warm")
         nc.vector.memset(zero[:], 0.0)
         nc.scalar.activation(warm[:], zero[:], TANH)
 
-        def minimum(piece):
-            nc.vector.tensor_tensor(smaller[:, cols(piece)], values[:].indirect(entries(piece)),
-                                    stream[:, cols(piece)], mybir.AluOpType.min)
+        def minimum(span):
+            nc.vector.tensor_tensor(smaller[:, span], values[:].indirect(entries(span)), stream[:, span],
+                                    mybir.AluOpType.min)
 
         def multiply_and_store(span):
             nc.vector.tensor_tensor(product[:, span], smaller[:, span], gate[:, span], mybir.AluOpType.mult)
             nc.sync.dma_start(out[:, span], product[:, span])
 
-        for piece in range(pieces):
-            nc.scalar.activation(gate[:, cols(piece)], gates[:].indirect(entries(piece)), TANH)
-        for piece in range(pieces - 1):
-            minimum(piece)
-        multiply_and_store(cols(0))
-        minimum(pieces - 1)
-        for piece in range(1, pieces - 1):
-            multiply_and_store(cols(piece))
+        for piece in pieces:
+            nc.scalar.activation(gate[:, piece], gates[:].indirect(entries(piece)), TANH)
+        minimum(early)
+        minimum(middle)
+        multiply_and_store(pieces[0])
+        minimum(late)
+        for piece in pieces[1:-1]:
+            multiply_and_store(piece)
         multiply_and_store(slice(n - PIECE, n - PIECE // 2))
         multiply_and_store(slice(n - PIECE // 2, n))

import concourse.mybir as mybir

F32 = mybir.dt.float32
U16 = mybir.dt.uint16
TANH = mybir.ActivationFunctionType.Tanh
LANES = 16
PIECE = 512
EARLY = 768


def tile_lookup_vg_mintanh_out_kernel(tc, tab, y, offs, out):
    nc = tc.nc
    rows, n = y.shape
    places = tab.shape[2]
    pieces = [slice(start, start + PIECE) for start in range(0, n, PIECE)]
    early, middle, late = slice(0, EARLY), slice(EARLY, EARLY + PIECE), slice(EARLY + PIECE, n)
    with tc.tile_pool(name="held", bufs=1) as held:
        offsets = held.tile([rows, n // LANES], U16, name="offsets")
        values = held.tile([rows, places], F32, name="values")
        gates = held.tile([rows, places], F32, name="gates")
        stream = held.tile([rows, n], F32, name="stream")
        smaller = held.tile([rows, n], F32, name="smaller")
        gate = held.tile([rows, n], F32, name="gate")
        product = held.tile([rows, n], F32, name="product")

        def entries(span):
            return offsets[:, span.start // LANES : span.stop // LANES]

        nc.sync.dma_start(values[:], tab[0])
        nc.sync.dma_start(offsets[:], offs)
        nc.sync.dma_start(stream[:, early], y[:, early])
        nc.sync.dma_start(gates[:], tab[1])
        nc.sync.dma_start(stream[:, middle], y[:, middle])
        nc.sync.dma_start(stream[:, late], y[:, late])

        zero = held.tile([rows, 1], F32, name="zero")
        warm = held.tile([rows, 1], F32, name="warm")
        nc.vector.memset(zero[:], 0.0)
        nc.scalar.activation(warm[:], zero[:], TANH)

        def minimum(span):
            nc.vector.tensor_tensor(smaller[:, span], values[:].indirect(entries(span)), stream[:, span],
                                    mybir.AluOpType.min)

        def multiply_and_store(span):
            nc.vector.tensor_tensor(product[:, span], smaller[:, span], gate[:, span], mybir.AluOpType.mult)
            nc.sync.dma_start(out[:, span], product[:, span])

        for piece in pieces:
            nc.scalar.activation(gate[:, piece], gates[:].indirect(entries(piece)), TANH)
        minimum(early)
        minimum(middle)
        multiply_and_store(pieces[0])
        minimum(late)
        for piece in pieces[1:-1]:
            multiply_and_store(piece)
        multiply_and_store(slice(n - PIECE, n - PIECE // 2))
        multiply_and_store(slice(n - PIECE // 2, n))
